import numpy as np
import ml_dtypes


def mxq(x, axis, fmt="e4m3"):
    dtype, down = {"e4m3": (ml_dtypes.float8_e4m3fn, 7), "e5m2": (ml_dtypes.float8_e5m2, 14)}[fmt]
    v = np.moveaxis(np.asarray(x, np.float32).astype(ml_dtypes.bfloat16).astype(np.float64), axis, -1)
    blocks = v.reshape(v.shape[:-1] + (-1, 32))
    amax = np.abs(blocks).max(-1, keepdims=True)
    byte = np.maximum(np.where(amax > 0, np.frexp(amax)[1] - 1 + 127, 0) - down, 1)
    scale = np.exp2(byte - 127.0)
    codes = (blocks / scale).astype(np.float32).astype(dtype).astype(np.float64)
    return np.moveaxis((codes * scale).reshape(v.shape), -1, axis)


WIDE = False


def mx_kscale(k):
    if not WIDE:
        return np.ones(k)
    levels = np.array([10, -10, 5, -5, 0])
    if k % 512:
        return np.exp2(np.random.permutation(np.resize(levels, k // 32))).repeat(32)
    a = np.empty((k // 512, 16))
    for p in range(k // 512):
        a[p, :8] = np.random.permutation(np.resize(levels, 8))
        for g in range(8):
            far = levels[np.abs(levels - a[p, g]) >= 10]
            a[p, g + 8] = far[np.random.randint(len(far))]
    return np.exp2(a.ravel()).repeat(32)


def f64(x):
    return np.asarray(x).astype(np.float64)


E2M1 = np.array([0.0, 0.5, 1.0, 1.5, 2.0, 3.0, 4.0, 6.0, -0.0, -0.5, -1.0, -1.5, -2.0, -3.0, -4.0, -6.0])


def pack_weight(w, fmt):
    k, n = w.shape
    w = f64(np.asarray(w, np.float32).astype(ml_dtypes.bfloat16)).reshape(k // 32, 32, n)
    amax = np.abs(w).max(1)
    if fmt == "e4m3":
        byte = np.frexp(amax)[1] - 1 + 127 - 7
    else:
        mant, ex = np.frexp(amax / 6.0)
        byte = np.where(mant > 0.5, ex, ex - 1) + 127
    byte = np.clip(np.where(amax > 0, byte, 1), 1, 254)
    scaled = (w * np.exp2(127.0 - byte)[:, None, :]).reshape(k, n).astype(np.float32)
    by_word = np.ascontiguousarray(scaled.reshape(k // 512, 128, 4, n).transpose(0, 1, 3, 2))
    if fmt == "e4m3":
        words = by_word.astype(ml_dtypes.float8_e4m3fn).view(np.uint8)
    else:
        c = by_word.astype(ml_dtypes.float4_e2m1fn).view(np.uint8) & 0xF
        words = (c[..., 0::2] | (c[..., 1::2] << 4)).reshape(k // 512, 128, 2 * n)
    return np.ascontiguousarray(words), np.ascontiguousarray(byte.astype(np.uint8).reshape(k // 512, 16, n))


def unpack_weight(words, scales, fmt):
    g, _, n = scales.shape
    words = np.ascontiguousarray(words).reshape(g, 128, n, -1)
    if fmt == "e4m3":
        vals = words.view(ml_dtypes.float8_e4m3fn).astype(np.float64)
    else:
        nib = np.empty((g, 128, n, 4), np.uint8)
        nib[..., 0::2] = words & 0xF
        nib[..., 1::2] = words >> 4
        vals = E2M1[nib]
    vals = vals * np.repeat(np.exp2(scales.astype(np.float64) - 127.0), 8, axis=1)[..., None]
    return vals.transpose(0, 1, 3, 2).reshape(g * 512, n)


def silu(v):
    return v / (1.0 + np.exp(-np.maximum(v, -700.0)))


O, K, M, T = 1024, 2560, 1024, 512


def setup_inputs():
    n = np.random.standard_normal
    s = mx_kscale(K)[:, None]
    x = n((K, T)); x[:O] *= 6.0
    w = n((K, M)) / np.sqrt(K) / s; w[:O] /= 2.0
    p_x4 = pack_weight(x[O:] * s[O:], "e2m1")
    p_w4 = pack_weight(w[O:], "e2m1")
    return {
        "x8": (x[:O] * s[:O]).astype(np.float32),
        "w8": (w[:O]).astype(np.float32),
        "x4_words": p_x4[0],
        "x4_scales": p_x4[1],
        "w4_words": p_w4[0],
        "w4_scales": p_w4[1],
        "b": (0.3 * n(1024)).astype(np.float32),
    }


def reference(x8, w8, x4_words, x4_scales, w4_words, w4_scales, b):
    x8_ = mxq(f64(x8), 0, "e4m3")
    w8_ = mxq(f64(w8), 0, "e4m3")
    x4_ = unpack_weight(x4_words, x4_scales, "e2m1")
    w4_ = unpack_weight(w4_words, w4_scales, "e2m1")
    y = x8_.T @ w8_ + x4_.T @ w4_
    return silu(y + f64(b)[None, :])

@@ -1,0 +1,169 @@
+from contextlib import ExitStack
+
+import concourse.mybir as mybir
+from concourse.masks import make_identity
+
+F32 = mybir.dt.float32
+BF16 = mybir.dt.bfloat16
+I32 = mybir.dt.int32
+U32 = mybir.dt.uint32
+U8 = mybir.dt.uint8
+FP8X4 = mybir.dt.float8_e4m3fn_x4
+FP4X4 = mybir.dt.float4_e2m1fn_x4
+SILU = mybir.ActivationFunctionType.Silu
+
+P = 128
+PACK = 4
+K_PASS = P * PACK
+T, N = 512, 1024
+K8, K4 = 1024, 1536
+G8, G4 = K8 // K_PASS, K4 // K_PASS
+TT = T // P
+
+FLOPS = 2 * (K8 + K4) * T * N
+
+CHUNKS = [256,256,256,256]
+
+
+def interleave(copy, grouped, raw, c0, c1):
+    copy(
+        out=grouped[:, c0:c1, :].rearrange("p (c i) j -> p c j i", i=4),
+        in_=raw[:, :, c0:c1].rearrange("p j (c i) -> p c j i", i=4),
+    )
+
+
+def tile_mix_atom_tm_silu_kernel(tc, x8, w8, x4_words, x4_scales, w4_words, w4_scales, b, out):
+    nc = tc.nc
+    with ExitStack() as ctx:
+        sb = ctx.enter_context(tc.tile_pool(name="sb", bufs=1))
+        psum = ctx.enter_context(tc.psum_pool(name="psum", bufs=2))
+        ctx.enter_context(tc.manual_schedule())
+
+        starts = [sum(CHUNKS[:c]) for c in range(len(CHUNKS))]
+
+        x_raw = [sb.tile([P, PACK, T], F32, name="x_raw%d" % g) for g in range(G8)]
+        x_grp = [sb.tile([P, T, PACK], BF16, name="x_grp%d" % g, align_bytes=64) for g in range(G8)]
+        x_cod = [sb.tile([P, T], U32, name="x_cod%d" % g, align_bytes=64) for g in range(G8)]
+        x_scl = [sb.tile([P, T], U8, name="x_scl%d" % g, align_bytes=64) for g in range(G8)]
+        w_raw = [[sb.tile([P, PACK, CHUNKS[c]], F32, name="w_raw%d_%d" % (c, g)) for g in range(G8)] for c in range(len(CHUNKS))]
+        w_grp = [[sb.tile([P, CHUNKS[c], PACK], BF16, name="w_grp%d_%d" % (c, g), align_bytes=64) for g in range(G8)] for c in range(len(CHUNKS))]
+        w_cod = [[sb.tile([P, CHUNKS[c]], U32, name="w_cod%d_%d" % (c, g), align_bytes=64) for g in range(G8)] for c in range(len(CHUNKS))]
+        w_scl = [[sb.tile([P, CHUNKS[c]], U8, name="w_scl%d_%d" % (c, g), align_bytes=64) for g in range(G8)] for c in range(len(CHUNKS))]
+        x4w = sb.tile([P, G4, 2 * T], U8, name="x4w", align_bytes=64)
+        w4w = sb.tile([P, G4, 2 * N], U8, name="w4w", align_bytes=64)
+        x4s = sb.tile([P, G4, T], U8, name="x4s", align_bytes=64)
+        w4s = sb.tile([P, G4, N], U8, name="w4s", align_bytes=64)
+        b_col = sb.tile([P, N // P], F32, name="b_col")
+        ident = sb.tile([P, P], F32, name="ident")
+        bias = sb.tile([P, N], F32, name="bias")
+        junk = sb.tile([P, 1], F32, name="junk")
+        junk2 = sb.tile([P, 1], F32, name="junk2")
+
+        nc.vector.memset(x4s[:].rearrange("p a n -> p (a n)").bitcast(I32), 0)
+        nc.vector.memset(w4s[:].rearrange("p a n -> p (a n)").bitcast(I32), 0)
+        nc.vector.memset(junk[:], 0.0)
+
+        x8_v = x8.rearrange("(g p j) t -> g p j t", p=P, j=PACK)
+        w8_v = w8.rearrange("(g p j) n -> g p j n", p=P, j=PACK)
+        ws_v = w4_scales.rearrange("a (q r) n -> r q a n", r=4)
+        xs_v = x4_scales.rearrange("a (q r) n -> r q a n", r=4)
+
+        nc.sync.dma_start(out=x4w[:], in_=x4_words.rearrange("a p n -> p a n"))
+        nc.sync.dma_start(out=w4w[:], in_=w4_words.rearrange("a p n -> p a n"))
+        for r in range(4):
+            queue = nc.scalar if r < 3 else nc.gpsimd
+            queue.dma_start(out=x4s[r:P:32, :, :].bitcast(I32), in_=xs_v[r].bitcast(I32))
+        nc.gpsimd.dma_start(out=b_col[:], in_=b.rearrange("(p c) -> p c", p=P))
+        make_identity(nc, ident[:])
+        for r in range(4):
+            nc.scalar.dma_start(out=w4s[r:P:32, :, :].bitcast(I32), in_=ws_v[r].bitcast(I32))
+        nc.sync.dma_start(out=x_raw[0][:], in_=x8_v[0])
+        nc.sync.dma_start(out=x_raw[1][:], in_=x8_v[1])
+        for c in range(len(CHUNKS)):
+            for g in range(G8):
+                nc.sync.dma_start(out=w_raw[c][g][:], in_=w8_v[g][:, :, starts[c] : starts[c] + CHUNKS[c]])
+
+        nc.scalar.activation(out=junk2[:], in_=junk[:], func=SILU)
+
+        for h in range(2):
+            bp = psum.tile([P, 4, P], F32, name="bp%d" % h, tag="t%d" % h)
+            for c in range(4):
+                nc.tensor.transpose(bp[:, c, :], b_col[:, 4 * h + c : 4 * h + c + 1].to_broadcast([P, P]), ident[:])
+            nc.scalar.copy(
+                out=bias[:].rearrange("q (p c) -> q p c", c=8)[:, :, 4 * h : 4 * h + 4],
+                in_=bp[:].rearrange("q c p -> q p c"),
+            )
+
+        for g in range(G8):
+            interleave(nc.vector.tensor_copy, x_grp[g], x_raw[g], 0, 256)
+            interleave(nc.scalar.copy, x_grp[g], x_raw[g], 256, T)
+            nc.vector.quantize_mx(out=x_cod[g][:].bitcast(FP8X4), scales=x_scl[g][:], in_=x_grp[g][:].rearrange("p t j -> p (t j)"))
+
+        acc = [[None] * TT for c in range(len(CHUNKS))]
+
+        def passes4(c):
+            n0, w = starts[c], CHUNKS[c]
+            for t in range(TT):
+                a_t = psum.tile([P, w], F32, name="acc%d_%d" % (c, t), tag="t%d" % t)
+                acc[c][t] = a_t
+                for a in range(G4):
+                    nc.tensor.matmul_mx(
+                        out=a_t[:],
+                        lhsT=x4w[:, a, 2 * P * t : 2 * P * (t + 1)].bitcast(FP4X4),
+                        lhsT_scale=x4s[:, a, P * t : P * (t + 1)],
+                        rhs=w4w[:, a, 2 * n0 : 2 * (n0 + w)].bitcast(FP4X4),
+                        rhs_scale=w4s[:, a, n0 : n0 + w],
+                        start=(a == 0),
+                        stop=False,
+                    )
+
+        def passes8(c, g):
+            for t in range(TT):
+                nc.tensor.matmul_mx(
+                    out=acc[c][t][:],
+                    lhsT=x_cod[g][:, P * t : P * (t + 1)].bitcast(FP8X4),
+                    lhsT_scale=x_scl[g][:, P * t : P * (t + 1)],
+                    rhs=w_cod[c][g][:].bitcast(FP8X4),
+                    rhs_scale=w_scl[c][g][:],
+                    start=False,
+                    stop=(g == G8 - 1),
+                )
+
+        def load_copy(c, g):
+            w = CHUNKS[c]
+            v = w * 8 // 16
+            interleave(nc.vector.tensor_copy, w_grp[c][g], w_raw[c][g], 0, v)
+            interleave(nc.scalar.copy, w_grp[c][g], w_raw[c][g], v, w)
+
+        def quant(c, g):
+            nc.vector.quantize_mx(out=w_cod[c][g][:].bitcast(FP8X4), scales=w_scl[c][g][:], in_=w_grp[c][g][:].rearrange("p n j -> p (n j)"))
+
+        def finish(c, t):
+            n0, w = starts[c], CHUNKS[c]
+            z = sb.tile([P, w], F32, name="z%d_%d" % (c, t))
+            y = sb.tile([P, w], F32, name="y%d_%d" % (c, t))
+            nc.vector.tensor_add(out=z[:], in0=acc[c][t][:], in1=bias[:, n0 : n0 + w])
+            nc.scalar.activation(out=y[:], in_=z[:], func=SILU)
+            nc.sync.dma_start(out=out[P * t : P * (t + 1), n0 : n0 + w], in_=y[:])
+
+        passes4(0)
+        passes4(1)
+        for c in range(len(CHUNKS)):
+            load_copy(c, 0)
+            if c > 0:
+                finish(c - 1, 0)
+            quant(c, 0)
+            passes8(c, 0)
+            if c > 0:
+                for t in range(1, 3):
+                    finish(c - 1, t)
+            load_copy(c, 1)
+            if c > 0:
+                for t in range(3, TT):
+                    finish(c - 1, t)
+            quant(c, 1)
+            passes8(c, 1)
+            if 0 < c < len(CHUNKS) - 1:
+                passes4(c + 1)
+        for t in range(TT):
+            finish(len(CHUNKS) - 1, t)

@@ -68,16 +68,16 @@ def tile_mix_atom_tm_silu_kernel(tc, x8, w8, x4_words, x4_scales, w4_words, w4_s
         ws_v = w4_scales.rearrange("a (q r) n -> r q a n", r=4)
         xs_v = x4_scales.rearrange("a (q r) n -> r q a n", r=4)
 
-        nc.sync.dma_start(out=x4w[:], in_=x4_words.rearrange("a p n -> p a n"))
-        nc.sync.dma_start(out=w4w[:], in_=w4_words.rearrange("a p n -> p a n"))
-        for r in range(4):
-            queue = nc.scalar if r < 3 else nc.gpsimd
-            queue.dma_start(out=x4s[r:P:32, :, :].bitcast(I32), in_=xs_v[r].bitcast(I32))
         nc.gpsimd.dma_start(out=b_col[:], in_=b.rearrange("(p c) -> p c", p=P))
         make_identity(nc, ident[:])
+        nc.sync.dma_start(out=x4w[:], in_=x4_words.rearrange("a p n -> p a n"))
+        nc.sync.dma_start(out=w4w[:], in_=w4_words.rearrange("a p n -> p a n"))
+        nc.sync.dma_start(out=x_raw[0][:], in_=x8_v[0])
+        nc.scalar.dma_start(out=x4s[0:P:32, :, :].bitcast(I32), in_=xs_v[0].bitcast(I32))
         for r in range(4):
             nc.scalar.dma_start(out=w4s[r:P:32, :, :].bitcast(I32), in_=ws_v[r].bitcast(I32))
-        nc.sync.dma_start(out=x_raw[0][:], in_=x8_v[0])
+        for r in range(1, 4):
+            nc.gpsimd.dma_start(out=x4s[r:P:32, :, :].bitcast(I32), in_=xs_v[r].bitcast(I32))
         nc.sync.dma_start(out=x_raw[1][:], in_=x8_v[1])
         for c in range(len(CHUNKS)):
             for g in range(G8):
@@ -155,15 +155,15 @@ def tile_mix_atom_tm_silu_kernel(tc, x8, w8, x4_words, x4_scales, w4_words, w4_s
             quant(c, 0)
             passes8(c, 0)
             if c > 0:
-                for t in range(1, 3):
+                for t in range(1, 2):
                     finish(c - 1, t)
             load_copy(c, 1)
             if c > 0:
-                for t in range(3, TT):
+                for t in range(2, TT):
                     finish(c - 1, t)
-            quant(c, 1)
-            passes8(c, 1)
             if 0 < c < len(CHUNKS) - 1:
                 passes4(c + 1)
+            quant(c, 1)
+            passes8(c, 1)
         for t in range(TT):
             finish(len(CHUNKS) - 1, t)

@@ -22,7 +22,8 @@ TT = T // P
 
 FLOPS = 2 * (K8 + K4) * T * N
 
-CHUNKS = [256,256,256,256]
+CHUNKS = [256,512,256]
+STORE_GROUPS = [[0],[1],[2]]
 
 
 def interleave(copy, grouped, raw, c0, c1):
@@ -60,43 +61,34 @@ def tile_mix_atom_tm_silu_kernel(tc, x8, w8, x4_words, x4_scales, w4_words, w4_s
         junk2 = sb.tile([P, 1], F32, name="junk2")
 
         nc.vector.memset(x4s[:].rearrange("p a n -> p (a n)").bitcast(I32), 0)
-        nc.vector.memset(w4s[:].rearrange("p a n -> p (a n)").bitcast(I32), 0)
         nc.vector.memset(junk[:], 0.0)
+        nc.vector.memset(w4s[:].rearrange("p a n -> p (a n)").bitcast(I32), 0)
 
         x8_v = x8.rearrange("(g p j) t -> g p j t", p=P, j=PACK)
         w8_v = w8.rearrange("(g p j) n -> g p j n", p=P, j=PACK)
         ws_v = w4_scales.rearrange("a (q r) n -> r q a n", r=4)
         xs_v = x4_scales.rearrange("a (q r) n -> r q a n", r=4)
 
-        nc.gpsimd.dma_start(out=b_col[:], in_=b.rearrange("(p c) -> p c", p=P))
         make_identity(nc, ident[:])
+        for r in range(4):
+            nc.scalar.dma_start(out=x4s[r:P:32, :, :].bitcast(I32), in_=xs_v[r].bitcast(I32))
+        for r in range(2):
+            nc.scalar.dma_start(out=w4s[r:P:32, :, :].bitcast(I32), in_=ws_v[r].bitcast(I32))
+        for r in range(2, 4):
+            nc.gpsimd.dma_start(out=w4s[r:P:32, :, :].bitcast(I32), in_=ws_v[r].bitcast(I32))
+        nc.gpsimd.dma_start(out=b_col[:], in_=b.rearrange("(p c) -> p c", p=P))
         nc.sync.dma_start(out=x4w[:], in_=x4_words.rearrange("a p n -> p a n"))
         nc.sync.dma_start(out=w4w[:], in_=w4_words.rearrange("a p n -> p a n"))
         nc.sync.dma_start(out=x_raw[0][:], in_=x8_v[0])
-        nc.scalar.dma_start(out=x4s[0:P:32, :, :].bitcast(I32), in_=xs_v[0].bitcast(I32))
-        for r in range(4):
-            nc.scalar.dma_start(out=w4s[r:P:32, :, :].bitcast(I32), in_=ws_v[r].bitcast(I32))
-        for r in range(1, 4):
-            nc.gpsimd.dma_start(out=x4s[r:P:32, :, :].bitcast(I32), in_=xs_v[r].bitcast(I32))
         nc.sync.dma_start(out=x_raw[1][:], in_=x8_v[1])
+        nc.scalar.activation(out=junk2[:], in_=junk[:], func=SILU)
         for c in range(len(CHUNKS)):
             for g in range(G8):
                 nc.sync.dma_start(out=w_raw[c][g][:], in_=w8_v[g][:, :, starts[c] : starts[c] + CHUNKS[c]])
 
-        nc.scalar.activation(out=junk2[:], in_=junk[:], func=SILU)
-
-        for h in range(2):
-            bp = psum.tile([P, 4, P], F32, name="bp%d" % h, tag="t%d" % h)
-            for c in range(4):
-                nc.tensor.transpose(bp[:, c, :], b_col[:, 4 * h + c : 4 * h + c + 1].to_broadcast([P, P]), ident[:])
-            nc.scalar.copy(
-                out=bias[:].rearrange("q (p c) -> q p c", c=8)[:, :, 4 * h : 4 * h + 4],
-                in_=bp[:].rearrange("q c p -> q p c"),
-            )
-
         for g in range(G8):
-            interleave(nc.vector.tensor_copy, x_grp[g], x_raw[g], 0, 256)
-            interleave(nc.scalar.copy, x_grp[g], x_raw[g], 256, T)
+            interleave(nc.vector.tensor_copy, x_grp[g], x_raw[g], 0, 320)
+            interleave(nc.scalar.copy, x_grp[g], x_raw[g], 320, T)
             nc.vector.quantize_mx(out=x_cod[g][:].bitcast(FP8X4), scales=x_scl[g][:], in_=x_grp[g][:].rearrange("p t j -> p (t j)"))
 
         acc = [[None] * TT for c in range(len(CHUNKS))]
@@ -131,22 +123,38 @@ def tile_mix_atom_tm_silu_kernel(tc, x8, w8, x4_words, x4_scales, w4_words, w4_s
 
         def load_copy(c, g):
             w = CHUNKS[c]
-            v = w * 8 // 16
+            v = w * 10 // 16
             interleave(nc.vector.tensor_copy, w_grp[c][g], w_raw[c][g], 0, v)
             interleave(nc.scalar.copy, w_grp[c][g], w_raw[c][g], v, w)
 
         def quant(c, g):
             nc.vector.quantize_mx(out=w_cod[c][g][:].bitcast(FP8X4), scales=w_scl[c][g][:], in_=w_grp[c][g][:].rearrange("p n j -> p (n j)"))
 
+        out_tiles = {}
+
         def finish(c, t):
             n0, w = starts[c], CHUNKS[c]
             z = sb.tile([P, w], F32, name="z%d_%d" % (c, t))
-            y = sb.tile([P, w], F32, name="y%d_%d" % (c, t))
             nc.vector.tensor_add(out=z[:], in0=acc[c][t][:], in1=bias[:, n0 : n0 + w])
-            nc.scalar.activation(out=y[:], in_=z[:], func=SILU)
-            nc.sync.dma_start(out=out[P * t : P * (t + 1), n0 : n0 + w], in_=y[:])
+            group = [k for k in STORE_GROUPS if c in k][0]
+            g0, gw = starts[group[0]], sum(CHUNKS[k] for k in group)
+            if c == group[0]:
+                out_tiles[t] = sb.tile([P, gw], F32, name="y%d_%d" % (c, t))
+            y = out_tiles[t]
+            nc.scalar.activation(out=y[:, n0 - g0 : n0 - g0 + w], in_=z[:], func=SILU)
+            if c == group[-1]:
+                nc.sync.dma_start(out=out[P * t : P * (t + 1), g0 : g0 + gw], in_=y[:])
 
         passes4(0)
+        for h in range(2):
+            bp = psum.tile([P, 4, P], F32, name="bp%d" % h, tag="t%d" % h)
+            for c in range(4):
+                nc.tensor.transpose(bp[:, c, :], b_col[:, 4 * h + c : 4 * h + c + 1].to_broadcast([P, P]), ident[:])
+            nc.scalar.copy(
+                out=bias[:].rearrange("q (p c) -> q p c", c=8)[:, :, 4 * h : 4 * h + 4],
+                in_=bp[:].rearrange("q c p -> q p c"),
+            )
+
         passes4(1)
         for c in range(len(CHUNKS)):
             load_copy(c, 0)

@@ -23,6 +23,8 @@ TT = T // P
 FLOPS = 2 * (K8 + K4) * T * N
 
 CHUNKS = [256,512,256]
+V_COLS = [[160,160],[320,320],[160,160]]
+PIECES = [[(0, 0)], [(0, 1)], [(1, 0), (2, 0)], [(1, 1)], [(2, 1)]]
 STORE_GROUPS = [[0],[1],[2]]
 
 
@@ -46,7 +48,7 @@ def tile_mix_atom_tm_silu_kernel(tc, x8, w8, x4_words, x4_scales, w4_words, w4_s
         x_grp = [sb.tile([P, T, PACK], BF16, name="x_grp%d" % g, align_bytes=64) for g in range(G8)]
         x_cod = [sb.tile([P, T], U32, name="x_cod%d" % g, align_bytes=64) for g in range(G8)]
         x_scl = [sb.tile([P, T], U8, name="x_scl%d" % g, align_bytes=64) for g in range(G8)]
-        w_raw = [[sb.tile([P, PACK, CHUNKS[c]], F32, name="w_raw%d_%d" % (c, g)) for g in range(G8)] for c in range(len(CHUNKS))]
+        w_src = {}
         w_grp = [[sb.tile([P, CHUNKS[c], PACK], BF16, name="w_grp%d_%d" % (c, g), align_bytes=64) for g in range(G8)] for c in range(len(CHUNKS))]
         w_cod = [[sb.tile([P, CHUNKS[c]], U32, name="w_cod%d_%d" % (c, g), align_bytes=64) for g in range(G8)] for c in range(len(CHUNKS))]
         w_scl = [[sb.tile([P, CHUNKS[c]], U8, name="w_scl%d_%d" % (c, g), align_bytes=64) for g in range(G8)] for c in range(len(CHUNKS))]
@@ -69,6 +71,7 @@ def tile_mix_atom_tm_silu_kernel(tc, x8, w8, x4_words, x4_scales, w4_words, w4_s
         ws_v = w4_scales.rearrange("a (q r) n -> r q a n", r=4)
         xs_v = x4_scales.rearrange("a (q r) n -> r q a n", r=4)
 
+        nc.gpsimd.dma_start(out=b_col[:], in_=b.rearrange("(p c) -> p c", p=P))
         make_identity(nc, ident[:])
         for r in range(4):
             nc.scalar.dma_start(out=x4s[r:P:32, :, :].bitcast(I32), in_=xs_v[r].bitcast(I32))
@@ -76,76 +79,25 @@ def tile_mix_atom_tm_silu_kernel(tc, x8, w8, x4_words, x4_scales, w4_words, w4_s
             nc.scalar.dma_start(out=w4s[r:P:32, :, :].bitcast(I32), in_=ws_v[r].bitcast(I32))
         for r in range(2, 4):
             nc.gpsimd.dma_start(out=w4s[r:P:32, :, :].bitcast(I32), in_=ws_v[r].bitcast(I32))
-        nc.gpsimd.dma_start(out=b_col[:], in_=b.rearrange("(p c) -> p c", p=P))
-        nc.sync.dma_start(out=x4w[:], in_=x4_words.rearrange("a p n -> p a n"))
-        nc.sync.dma_start(out=w4w[:], in_=w4_words.rearrange("a p n -> p a n"))
         nc.sync.dma_start(out=x_raw[0][:], in_=x8_v[0])
         nc.sync.dma_start(out=x_raw[1][:], in_=x8_v[1])
+        nc.sync.dma_start(out=x4w[:], in_=x4_words.rearrange("a p n -> p a n"))
+        nc.sync.dma_start(out=w4w[:], in_=w4_words.rearrange("a p n -> p a n"))
         nc.scalar.activation(out=junk2[:], in_=junk[:], func=SILU)
-        for c in range(len(CHUNKS)):
-            for g in range(G8):
-                nc.sync.dma_start(out=w_raw[c][g][:], in_=w8_v[g][:, :, starts[c] : starts[c] + CHUNKS[c]])
+        for piece in PIECES:
+            g = piece[0][1]
+            n0, n1 = starts[piece[0][0]], starts[piece[-1][0]] + CHUNKS[piece[-1][0]]
+            raw = sb.tile([P, PACK, n1 - n0], F32, name="w_raw%d_%d" % (piece[0][0], g))
+            for c, gg in piece:
+                w_src[(c, g)] = raw[:, :, starts[c] - n0 : starts[c] - n0 + CHUNKS[c]]
+            nc.sync.dma_start(out=raw[:], in_=w8_v[g][:, :, n0:n1])
 
-        for g in range(G8):
+        def prep_x(g):
             interleave(nc.vector.tensor_copy, x_grp[g], x_raw[g], 0, 320)
             interleave(nc.scalar.copy, x_grp[g], x_raw[g], 320, T)
             nc.vector.quantize_mx(out=x_cod[g][:].bitcast(FP8X4), scales=x_scl[g][:], in_=x_grp[g][:].rearrange("p t j -> p (t j)"))
 
-        acc = [[None] * TT for c in range(len(CHUNKS))]
-
-        def passes4(c):
-            n0, w = starts[c], CHUNKS[c]
-            for t in range(TT):
-                a_t = psum.tile([P, w], F32, name="acc%d_%d" % (c, t), tag="t%d" % t)
-                acc[c][t] = a_t
-                for a in range(G4):
-                    nc.tensor.matmul_mx(
-                        out=a_t[:],
-                        lhsT=x4w[:, a, 2 * P * t : 2 * P * (t + 1)].bitcast(FP4X4),
-                        lhsT_scale=x4s[:, a, P * t : P * (t + 1)],
-                        rhs=w4w[:, a, 2 * n0 : 2 * (n0 + w)].bitcast(FP4X4),
-                        rhs_scale=w4s[:, a, n0 : n0 + w],
-                        start=(a == 0),
-                        stop=False,
-                    )
-
-        def passes8(c, g):
-            for t in range(TT):
-                nc.tensor.matmul_mx(
-                    out=acc[c][t][:],
-                    lhsT=x_cod[g][:, P * t : P * (t + 1)].bitcast(FP8X4),
-                    lhsT_scale=x_scl[g][:, P * t : P * (t + 1)],
-                    rhs=w_cod[c][g][:].bitcast(FP8X4),
-                    rhs_scale=w_scl[c][g][:],
-                    start=False,
-                    stop=(g == G8 - 1),
-                )
-
-        def load_copy(c, g):
-            w = CHUNKS[c]
-            v = w * 10 // 16
-            interleave(nc.vector.tensor_copy, w_grp[c][g], w_raw[c][g], 0, v)
-            interleave(nc.scalar.copy, w_grp[c][g], w_raw[c][g], v, w)
-
-        def quant(c, g):
-            nc.vector.quantize_mx(out=w_cod[c][g][:].bitcast(FP8X4), scales=w_scl[c][g][:], in_=w_grp[c][g][:].rearrange("p n j -> p (n j)"))
-
-        out_tiles = {}
-
-        def finish(c, t):
-            n0, w = starts[c], CHUNKS[c]
-            z = sb.tile([P, w], F32, name="z%d_%d" % (c, t))
-            nc.vector.tensor_add(out=z[:], in0=acc[c][t][:], in1=bias[:, n0 : n0 + w])
-            group = [k for k in STORE_GROUPS if c in k][0]
-            g0, gw = starts[group[0]], sum(CHUNKS[k] for k in group)
-            if c == group[0]:
-                out_tiles[t] = sb.tile([P, gw], F32, name="y%d_%d" % (c, t))
-            y = out_tiles[t]
-            nc.scalar.activation(out=y[:, n0 - g0 : n0 - g0 + w], in_=z[:], func=SILU)
-            if c == group[-1]:
-                nc.sync.dma_start(out=out[P * t : P * (t + 1), g0 : g0 + gw], in_=y[:])
-
-        passes4(0)
+        prep_x(0)
         for h in range(2):
             bp = psum.tile([P, 4, P], F32, name="bp%d" % h, tag="t%d" % h)
             for c in range(4):
@@ -155,23 +107,101 @@ def tile_mix_atom_tm_silu_kernel(tc, x8, w8, x4_words, x4_scales, w4_words, w4_s
                 in_=bp[:].rearrange("q c p -> q p c"),
             )
 
-        passes4(1)
-        for c in range(len(CHUNKS)):
-            load_copy(c, 0)
-            if c > 0:
-                finish(c - 1, 0)
-            quant(c, 0)
-            passes8(c, 0)
-            if c > 0:
-                for t in range(1, 2):
-                    finish(c - 1, t)
-            load_copy(c, 1)
-            if c > 0:
-                for t in range(2, TT):
-                    finish(c - 1, t)
-            if 0 < c < len(CHUNKS) - 1:
-                passes4(c + 1)
-            quant(c, 1)
-            passes8(c, 1)
-        for t in range(TT):
-            finish(len(CHUNKS) - 1, t)
+        prep_x(1)
+
+        acc = [[None] * TT for c in range(len(CHUNKS))]
+
+        def bank(c, t):
+            if acc[c][t] is None:
+                a_t = psum.tile([P, CHUNKS[c]], F32, name="acc%d_%d" % (c, t), tag="t%d" % t)
+                acc[c][t] = a_t
+            return acc[c][t]
+
+        def passes4(c, a0, a1, first):
+            n0, w = starts[c], CHUNKS[c]
+            for t in range(TT):
+                for a in range(a0, a1):
+                    nc.tensor.matmul_mx(
+                        out=bank(c, t)[:],
+                        lhsT=x4w[:, a, 2 * P * t : 2 * P * (t + 1)].bitcast(FP4X4),
+                        lhsT_scale=x4s[:, a, P * t : P * (t + 1)],
+                        rhs=w4w[:, a, 2 * n0 : 2 * (n0 + w)].bitcast(FP4X4),
+                        rhs_scale=w4s[:, a, n0 : n0 + w],
+                        start=(first and a == a0),
+                        stop=False,
+                    )
+
+        def passes8(c, g, first):
+            for t in range(TT):
+                nc.tensor.matmul_mx(
+                    out=bank(c, t)[:],
+                    lhsT=x_cod[g][:, P * t : P * (t + 1)].bitcast(FP8X4),
+                    lhsT_scale=x_scl[g][:, P * t : P * (t + 1)],
+                    rhs=w_cod[c][g][:].bitcast(FP8X4),
+                    rhs_scale=w_scl[c][g][:],
+                    start=first,
+                    stop=(g == G8 - 1),
+                )
+
+        def vcopy(c, g):
+            interleave(nc.vector.tensor_copy, w_grp[c][g], w_src[(c, g)], 0, V_COLS[c][g])
+
+        def scopy(c, g):
+            interleave(nc.scalar.copy, w_grp[c][g], w_src[(c, g)], V_COLS[c][g], CHUNKS[c])
+
+        def quant(c, g):
+            nc.vector.quantize_mx(out=w_cod[c][g][:].bitcast(FP8X4), scales=w_scl[c][g][:], in_=w_grp[c][g][:].rearrange("p n j -> p (n j)"))
+
+        def finish(c, t, parts=1):
+            n0, w = starts[c], CHUNKS[c] // parts
+            for h in range(parts):
+                z = sb.tile([P, w], F32, name="z%d_%d_%d" % (c, t, h))
+                y = sb.tile([P, w], F32, name="y%d_%d_%d" % (c, t, h))
+                cols = slice(n0 + h * w, n0 + (h + 1) * w)
+                nc.vector.tensor_add(out=z[:], in0=acc[c][t][:, h * w : (h + 1) * w], in1=bias[:, cols])
+                nc.scalar.activation(out=y[:], in_=z[:], func=SILU)
+                nc.sync.dma_start(out=out[P * t : P * (t + 1), cols], in_=y[:])
+
+        passes4(0, 0, G4, True)
+        STEPS = [
+            (vcopy, 0, 0),
+            (scopy, 0, 0),
+            (quant, 0, 0),
+            (passes8, 0, 0, False),
+            (vcopy, 0, 1),
+            (scopy, 0, 1),
+            (quant, 0, 1),
+            (passes8, 0, 1, False),
+            (passes4, 1, 0, 3, True),
+            (finish, 0, 0),
+            (finish, 0, 1),
+            (vcopy, 1, 0),
+            (scopy, 1, 0),
+            (finish, 0, 2),
+            (quant, 1, 0),
+            (passes8, 1, 0, False),
+            (vcopy, 2, 0),
+            (scopy, 2, 0),
+            (finish, 0, 3),
+            (passes4, 2, 0, 3, True),
+            (quant, 2, 0),
+            (passes8, 2, 0, False),
+            (vcopy, 1, 1),
+            (scopy, 1, 1),
+            (quant, 1, 1),
+            (passes8, 1, 1, False),
+            (vcopy, 2, 1),
+            (scopy, 2, 1),
+            (finish, 1, 0),
+            (quant, 2, 1),
+            (passes8, 2, 1, False),
+            (finish, 1, 1),
+            (finish, 1, 2),
+            (finish, 1, 3),
+            (finish, 2, 0),
+            (finish, 2, 1),
+            (finish, 2, 2),
+            (finish, 2, 3),
+        ]
+        for step in STEPS:
+            step[0](*step[1:])

from contextlib import ExitStack

import concourse.mybir as mybir
from concourse.masks import make_identity

F32 = mybir.dt.float32
BF16 = mybir.dt.bfloat16
I32 = mybir.dt.int32
U32 = mybir.dt.uint32
U8 = mybir.dt.uint8
FP8X4 = mybir.dt.float8_e4m3fn_x4
FP4X4 = mybir.dt.float4_e2m1fn_x4
SILU = mybir.ActivationFunctionType.Silu

P = 128
PACK = 4
K_PASS = P * PACK
T, N = 512, 1024
K8, K4 = 1024, 1536
G8, G4 = K8 // K_PASS, K4 // K_PASS
TT = T // P

FLOPS = 2 * (K8 + K4) * T * N

CHUNKS = [256,512,256]
V_COLS = [[160,160],[320,320],[160,160]]
PIECES = [[(0, 0)], [(0, 1)], [(1, 0), (2, 0)], [(1, 1)], [(2, 1)]]
STORE_GROUPS = [[0],[1],[2]]


def interleave(copy, grouped, raw, c0, c1):
    copy(
        out=grouped[:, c0:c1, :].rearrange("p (c i) j -> p c j i", i=4),
        in_=raw[:, :, c0:c1].rearrange("p j (c i) -> p c j i", i=4),
    )


def tile_mix_atom_tm_silu_kernel(tc, x8, w8, x4_words, x4_scales, w4_words, w4_scales, b, out):
    nc = tc.nc
    with ExitStack() as ctx:
        sb = ctx.enter_context(tc.tile_pool(name="sb", bufs=1))
        psum = ctx.enter_context(tc.psum_pool(name="psum", bufs=2))
        ctx.enter_context(tc.manual_schedule())

        starts = [sum(CHUNKS[:c]) for c in range(len(CHUNKS))]

        x_raw = [sb.tile([P, PACK, T], F32, name="x_raw%d" % g) for g in range(G8)]
        x_grp = [sb.tile([P, T, PACK], BF16, name="x_grp%d" % g, align_bytes=64) for g in range(G8)]
        x_cod = [sb.tile([P, T], U32, name="x_cod%d" % g, align_bytes=64) for g in range(G8)]
        x_scl = [sb.tile([P, T], U8, name="x_scl%d" % g, align_bytes=64) for g in range(G8)]
        w_src = {}
        w_grp = [[sb.tile([P, CHUNKS[c], PACK], BF16, name="w_grp%d_%d" % (c, g), align_bytes=64) for g in range(G8)] for c in range(len(CHUNKS))]
        w_cod = [[sb.tile([P, CHUNKS[c]], U32, name="w_cod%d_%d" % (c, g), align_bytes=64) for g in range(G8)] for c in range(len(CHUNKS))]
        w_scl = [[sb.tile([P, CHUNKS[c]], U8, name="w_scl%d_%d" % (c, g), align_bytes=64) for g in range(G8)] for c in range(len(CHUNKS))]
        x4w = sb.tile([P, G4, 2 * T], U8, name="x4w", align_bytes=64)
        w4w = sb.tile([P, G4, 2 * N], U8, name="w4w", align_bytes=64)
        x4s = sb.tile([P, G4, T], U8, name="x4s", align_bytes=64)
        w4s = sb.tile([P, G4, N], U8, name="w4s", align_bytes=64)
        b_col = sb.tile([P, N // P], F32, name="b_col")
        ident = sb.tile([P, P], F32, name="ident")
        bias = sb.tile([P, N], F32, name="bias")
        junk = sb.tile([P, 1], F32, name="junk")
        junk2 = sb.tile([P, 1], F32, name="junk2")

        nc.vector.memset(x4s[:].rearrange("p a n -> p (a n)").bitcast(I32), 0)
        nc.vector.memset(junk[:], 0.0)
        nc.vector.memset(w4s[:].rearrange("p a n -> p (a n)").bitcast(I32), 0)

        x8_v = x8.rearrange("(g p j) t -> g p j t", p=P, j=PACK)
        w8_v = w8.rearrange("(g p j) n -> g p j n", p=P, j=PACK)
        ws_v = w4_scales.rearrange("a (q r) n -> r q a n", r=4)
        xs_v = x4_scales.rearrange("a (q r) n -> r q a n", r=4)

        nc.gpsimd.dma_start(out=b_col[:], in_=b.rearrange("(p c) -> p c", p=P))
        make_identity(nc, ident[:])
        for r in range(4):
            nc.scalar.dma_start(out=x4s[r:P:32, :, :].bitcast(I32), in_=xs_v[r].bitcast(I32))
        for r in range(2):
            nc.scalar.dma_start(out=w4s[r:P:32, :, :].bitcast(I32), in_=ws_v[r].bitcast(I32))
        for r in range(2, 4):
            nc.gpsimd.dma_start(out=w4s[r:P:32, :, :].bitcast(I32), in_=ws_v[r].bitcast(I32))
        nc.sync.dma_start(out=x_raw[0][:], in_=x8_v[0])
        nc.sync.dma_start(out=x_raw[1][:], in_=x8_v[1])
        nc.sync.dma_start(out=x4w[:], in_=x4_words.rearrange("a p n -> p a n"))
        nc.sync.dma_start(out=w4w[:], in_=w4_words.rearrange("a p n -> p a n"))
        nc.scalar.activation(out=junk2[:], in_=junk[:], func=SILU)
        for piece in PIECES:
            g = piece[0][1]
            n0, n1 = starts[piece[0][0]], starts[piece[-1][0]] + CHUNKS[piece[-1][0]]
            raw = sb.tile([P, PACK, n1 - n0], F32, name="w_raw%d_%d" % (piece[0][0], g))
            for c, gg in piece:
                w_src[(c, g)] = raw[:, :, starts[c] - n0 : starts[c] - n0 + CHUNKS[c]]
            nc.sync.dma_start(out=raw[:], in_=w8_v[g][:, :, n0:n1])

        def prep_x(g):
            interleave(nc.vector.tensor_copy, x_grp[g], x_raw[g], 0, 320)
            interleave(nc.scalar.copy, x_grp[g], x_raw[g], 320, T)
            nc.vector.quantize_mx(out=x_cod[g][:].bitcast(FP8X4), scales=x_scl[g][:], in_=x_grp[g][:].rearrange("p t j -> p (t j)"))

        prep_x(0)
        for h in range(2):
            bp = psum.tile([P, 4, P], F32, name="bp%d" % h, tag="t%d" % h)
            for c in range(4):
                nc.tensor.transpose(bp[:, c, :], b_col[:, 4 * h + c : 4 * h + c + 1].to_broadcast([P, P]), ident[:])
            nc.scalar.copy(
                out=bias[:].rearrange("q (p c) -> q p c", c=8)[:, :, 4 * h : 4 * h + 4],
                in_=bp[:].rearrange("q c p -> q p c"),
            )

        prep_x(1)

        acc = [[None] * TT for c in range(len(CHUNKS))]

        def bank(c, t):
            if acc[c][t] is None:
                a_t = psum.tile([P, CHUNKS[c]], F32, name="acc%d_%d" % (c, t), tag="t%d" % t)
                acc[c][t] = a_t
            return acc[c][t]

        def passes4(c, a0, a1, first):
            n0, w = starts[c], CHUNKS[c]
            for t in range(TT):
                for a in range(a0, a1):
                    nc.tensor.matmul_mx(
                        out=bank(c, t)[:],
                        lhsT=x4w[:, a, 2 * P * t : 2 * P * (t + 1)].bitcast(FP4X4),
                        lhsT_scale=x4s[:, a, P * t : P * (t + 1)],
                        rhs=w4w[:, a, 2 * n0 : 2 * (n0 + w)].bitcast(FP4X4),
                        rhs_scale=w4s[:, a, n0 : n0 + w],
                        start=(first and a == a0),
                        stop=False,
                    )

        def passes8(c, g, first):
            for t in range(TT):
                nc.tensor.matmul_mx(
                    out=bank(c, t)[:],
                    lhsT=x_cod[g][:, P * t : P * (t + 1)].bitcast(FP8X4),
                    lhsT_scale=x_scl[g][:, P * t : P * (t + 1)],
                    rhs=w_cod[c][g][:].bitcast(FP8X4),
                    rhs_scale=w_scl[c][g][:],
                    start=first,
                    stop=(g == G8 - 1),
                )

        def vcopy(c, g):
            interleave(nc.vector.tensor_copy, w_grp[c][g], w_src[(c, g)], 0, V_COLS[c][g])

        def scopy(c, g):
            interleave(nc.scalar.copy, w_grp[c][g], w_src[(c, g)], V_COLS[c][g], CHUNKS[c])

        def quant(c, g):
            nc.vector.quantize_mx(out=w_cod[c][g][:].bitcast(FP8X4), scales=w_scl[c][g][:], in_=w_grp[c][g][:].rearrange("p n j -> p (n j)"))

        def finish(c, t, parts=1):
            n0, w = starts[c], CHUNKS[c] // parts
            for h in range(parts):
                z = sb.tile([P, w], F32, name="z%d_%d_%d" % (c, t, h))
                y = sb.tile([P, w], F32, name="y%d_%d_%d" % (c, t, h))
                cols = slice(n0 + h * w, n0 + (h + 1) * w)
                nc.vector.tensor_add(out=z[:], in0=acc[c][t][:, h * w : (h + 1) * w], in1=bias[:, cols])
                nc.scalar.activation(out=y[:], in_=z[:], func=SILU)
                nc.sync.dma_start(out=out[P * t : P * (t + 1), cols], in_=y[:])

        passes4(0, 0, G4, True)
        STEPS = [
            (vcopy, 0, 0),
            (scopy, 0, 0),
            (quant, 0, 0),
            (passes8, 0, 0, False),
            (vcopy, 0, 1),
            (scopy, 0, 1),
            (quant, 0, 1),
            (passes8, 0, 1, False),
            (passes4, 1, 0, 3, True),
            (finish, 0, 0),
            (finish, 0, 1),
            (vcopy, 1, 0),
            (scopy, 1, 0),
            (finish, 0, 2),
            (quant, 1, 0),
            (passes8, 1, 0, False),
            (vcopy, 2, 0),
            (scopy, 2, 0),
            (finish, 0, 3),
            (passes4, 2, 0, 3, True),
            (quant, 2, 0),
            (passes8, 2, 0, False),
            (vcopy, 1, 1),
            (scopy, 1, 1),
            (quant, 1, 1),
            (passes8, 1, 1, False),
            (vcopy, 2, 1),
            (scopy, 2, 1),
            (finish, 1, 0),
            (quant, 2, 1),
            (passes8, 2, 1, False),
            (finish, 1, 1),
            (finish, 1, 2),
            (finish, 1, 3),
            (finish, 2, 0),
            (finish, 2, 1),
            (finish, 2, 2),
            (finish, 2, 3),
        ]
        for step in STEPS:
            step[0](*step[1:])
